import numpy as np
import ml_dtypes

BF16 = ml_dtypes.bfloat16


def bf(x):
    return np.asarray(x, np.float32).astype(BF16)


def f32(x):
    return np.asarray(x, np.float32)


def f64(x):
    return np.asarray(x).astype(np.float64)


def striped(idx):
    return np.tile(idx.reshape(-1, 16).T, (8, 1))


def rows(idx, k):
    return np.tile(idx, (k, 1))


def look(tab, idx):
    return np.take_along_axis(f64(tab), rows(idx, len(tab)), axis=1)


K, S, D, V, N, M = 512, 2048, 4, 512, 2048, 128


def setup_inputs():
    return {"tab": f32(np.random.standard_normal((K, S))), "x0": f32(np.random.standard_normal((K, V))), "w": bf(np.random.standard_normal((K, M)) / np.sqrt(K)), "offs": striped(np.random.permutation(S)[:N])}


def reference(tab, x0, w, offs):
    idx = offs[:16].T.reshape(-1)
    x = f64(x0)
    for d in range(D):
        x = np.maximum(x, look(tab, idx[d * V:(d + 1) * V]))
    y = f64(w).T @ x
    return y

@@ -1,0 +1,48 @@
+import concourse.mybir as mybir
+
+P = 128
+STRIPE = 16
+F32, BF16, U16 = mybir.dt.float32, mybir.dt.bfloat16, mybir.dt.uint16
+FLOPS = 2 * 512 * 128 * 512
+
+
+def tile_lookup_pool_max_none_kernel(tc, tab, x0, w, offs, out):
+    nc = tc.nc
+    rows, table_cols = tab.shape
+    width = x0.shape[1]
+    out_rows = w.shape[1]
+    blocks = rows // P
+    piece_cols = width // STRIPE
+    neighbours = offs.shape[1] // piece_cols
+    with (
+        tc.tile_pool(name="held", bufs=1) as held,
+        tc.tile_pool(name="work", bufs=2) as work,
+        tc.psum_pool(name="psum", bufs=1) as psum,
+    ):
+        offsets = held.tile([P, offs.shape[1]], U16, name="offsets")
+        nc.sync.dma_start(offsets[:], offs)
+        tables, centres = [], []
+        for b in range(blocks):
+            table = held.tile([P, table_cols], F32, name=f"table{b}")
+            centre = held.tile([P, width], F32, name=f"centre{b}")
+            nc.sync.dma_start(table[:], tab[b * P : (b + 1) * P, :])
+            nc.sync.dma_start(centre[:], x0[b * P : (b + 1) * P, :])
+            tables.append(table)
+            centres.append(centre)
+        weights = held.tile([P, blocks, out_rows], BF16, name="weights")
+        nc.sync.dma_start(weights[:], w.rearrange("(b p) m -> p b m", p=P))
+
+        product = psum.tile([out_rows, width], F32, name="product")
+        for b in range(blocks):
+            largest = centres[b]
+            for d in range(neighbours):
+                picked = tables[b][:].indirect(offsets[:, d * piece_cols : (d + 1) * piece_cols])
+                larger = work.tile([P, width], F32, name="larger")
+                nc.vector.tensor_tensor(larger[:], picked, largest[:], mybir.AluOpType.max)
+                largest = larger
+            rounded = work.tile([P, width], BF16, name="rounded")
+            nc.scalar.copy(rounded[:], largest[:])
+            nc.tensor.matmul(product[:], weights[:, b, :], rounded[:], start=b == 0, stop=b == blocks - 1)
+        result = held.tile([out_rows, width], F32, name="result")
+        nc.vector.tensor_copy(result[:], product[:])
+        nc.sync.dma_start(out, result[:])

@@ -4,6 +4,7 @@ P = 128
 STRIPE = 16
 F32, BF16, U16 = mybir.dt.float32, mybir.dt.bfloat16, mybir.dt.uint16
 FLOPS = 2 * 512 * 128 * 512
+HALVES = 2
 
 
 def tile_lookup_pool_max_none_kernel(tc, tab, x0, w, offs, out):
@@ -12,37 +13,45 @@ def tile_lookup_pool_max_none_kernel(tc, tab, x0, w, offs, out):
     width = x0.shape[1]
     out_rows = w.shape[1]
     blocks = rows // P
-    piece_cols = width // STRIPE
-    neighbours = offs.shape[1] // piece_cols
+    neighbours = offs.shape[1] * STRIPE // width
+    half = width // HALVES
     with (
         tc.tile_pool(name="held", bufs=1) as held,
-        tc.tile_pool(name="work", bufs=2) as work,
+        tc.tile_pool(name="work", bufs=neighbours) as work,
         tc.psum_pool(name="psum", bufs=1) as psum,
     ):
         offsets = held.tile([P, offs.shape[1]], U16, name="offsets")
-        nc.sync.dma_start(offsets[:], offs)
-        tables, centres = [], []
-        for b in range(blocks):
-            table = held.tile([P, table_cols], F32, name=f"table{b}")
-            centre = held.tile([P, width], F32, name=f"centre{b}")
-            nc.sync.dma_start(table[:], tab[b * P : (b + 1) * P, :])
-            nc.sync.dma_start(centre[:], x0[b * P : (b + 1) * P, :])
-            tables.append(table)
-            centres.append(centre)
         weights = held.tile([P, blocks, out_rows], BF16, name="weights")
-        nc.sync.dma_start(weights[:], w.rearrange("(b p) m -> p b m", p=P))
-
-        product = psum.tile([out_rows, width], F32, name="product")
+        tables = [held.tile([P, table_cols], F32, name=f"table{b}") for b in range(blocks)]
+        centres = [[held.tile([P, half], F32, name=f"centre{b}_{h}") for h in range(HALVES)] for b in range(blocks)]
+        nc.sync.dma_start(offsets[:], offs)
         for b in range(blocks):
-            largest = centres[b]
+            block_rows = slice(b * P, (b + 1) * P)
+            nc.sync.dma_start(tables[b][:], tab[block_rows, :])
+            for h in range(HALVES):
+                nc.sync.dma_start(centres[b][h][:], x0[block_rows, h * half : (h + 1) * half])
+            if b == 0:
+                nc.sync.dma_start(weights[:], w.rearrange("(b p) m -> p b m", p=P))
+
+        products = [psum.tile([out_rows, half], F32, name=f"product{h}") for h in range(HALVES)]
+        for b in range(blocks):
+            largest = list(centres[b])
             for d in range(neighbours):
-                picked = tables[b][:].indirect(offsets[:, d * piece_cols : (d + 1) * piece_cols])
-                larger = work.tile([P, width], F32, name="larger")
-                nc.vector.tensor_tensor(larger[:], picked, largest[:], mybir.AluOpType.max)
-                largest = larger
-            rounded = work.tile([P, width], BF16, name="rounded")
-            nc.scalar.copy(rounded[:], largest[:])
-            nc.tensor.matmul(product[:], weights[:, b, :], rounded[:], start=b == 0, stop=b == blocks - 1)
-        result = held.tile([out_rows, width], F32, name="result")
-        nc.vector.tensor_copy(result[:], product[:])
-        nc.sync.dma_start(out, result[:])
+                for h in range(HALVES):
+                    first = (d * width + h * half) // STRIPE
+                    picked = tables[b][:].indirect(offsets[:, first : first + half // STRIPE])
+                    larger = work.tile([P, half], F32, name=f"larger{h}")
+                    nc.vector.tensor_tensor(larger[:], picked, largest[h][:], mybir.AluOpType.max)
+                    largest[h] = larger
+            for h in range(HALVES):
+                rounded = work.tile([P, half], BF16, name=f"rounded{h}")
+                if b == blocks - 1 and h == HALVES - 1:
+                    nc.vector.tensor_copy(rounded[:], largest[h][:])
+                else:
+                    nc.scalar.copy(rounded[:], largest[h][:])
+                nc.tensor.matmul(products[h][:], weights[:, b, :], rounded[:], start=b == 0, stop=b == blocks - 1)
+        results = [held.tile([out_rows, half], F32, name=f"result{h}") for h in range(HALVES)]
+        nc.scalar.copy(results[0][:], products[0][:])
+        nc.scalar.dma_start(out[:, :half], results[0][:])
+        nc.vector.tensor_copy(results[1][:], products[1][:])
+        nc.sync.dma_start(out[:, half:], results[1][:])

@@ -5,6 +5,7 @@ STRIPE = 16
 F32, BF16, U16 = mybir.dt.float32, mybir.dt.bfloat16, mybir.dt.uint16
 FLOPS = 2 * 512 * 128 * 512
 HALVES = 2
+LAG = 2
 
 
 def tile_lookup_pool_max_none_kernel(tc, tab, x0, w, offs, out):
@@ -15,43 +16,52 @@ def tile_lookup_pool_max_none_kernel(tc, tab, x0, w, offs, out):
     blocks = rows // P
     neighbours = offs.shape[1] * STRIPE // width
     half = width // HALVES
+    halves = [slice(h * half, (h + 1) * half) for h in range(HALVES)]
     with (
         tc.tile_pool(name="held", bufs=1) as held,
-        tc.tile_pool(name="work", bufs=neighbours) as work,
         tc.psum_pool(name="psum", bufs=1) as psum,
     ):
         offsets = held.tile([P, offs.shape[1]], U16, name="offsets")
         weights = held.tile([P, blocks, out_rows], BF16, name="weights")
         tables = [held.tile([P, table_cols], F32, name=f"table{b}") for b in range(blocks)]
-        centres = [[held.tile([P, half], F32, name=f"centre{b}_{h}") for h in range(HALVES)] for b in range(blocks)]
+        centres = [held.tile([P, width], F32, name=f"centre{b}") for b in range(blocks)]
         nc.sync.dma_start(offsets[:], offs)
         for b in range(blocks):
             block_rows = slice(b * P, (b + 1) * P)
             nc.sync.dma_start(tables[b][:], tab[block_rows, :])
-            for h in range(HALVES):
-                nc.sync.dma_start(centres[b][h][:], x0[block_rows, h * half : (h + 1) * half])
-            if b == 0:
+            nc.sync.dma_start(centres[b][:], x0[block_rows, :])
+            if b == 1:
                 nc.sync.dma_start(weights[:], w.rearrange("(b p) m -> p b m", p=P))
 
         products = [psum.tile([out_rows, half], F32, name=f"product{h}") for h in range(HALVES)]
-        for b in range(blocks):
-            largest = list(centres[b])
-            for d in range(neighbours):
-                for h in range(HALVES):
-                    first = (d * width + h * half) // STRIPE
-                    picked = tables[b][:].indirect(offsets[:, first : first + half // STRIPE])
-                    larger = work.tile([P, half], F32, name=f"larger{h}")
-                    nc.vector.tensor_tensor(larger[:], picked, largest[h][:], mybir.AluOpType.max)
-                    largest[h] = larger
-            for h in range(HALVES):
-                rounded = work.tile([P, half], BF16, name=f"rounded{h}")
-                if b == blocks - 1 and h == HALVES - 1:
-                    nc.vector.tensor_copy(rounded[:], largest[h][:])
+        largest = list(centres)
+        for step in range(LAG * (blocks - 1) + neighbours):
+            active = [b for b in reversed(range(blocks)) if 0 <= step - LAG * b < neighbours]
+            parts = halves if len(active) == 1 else [slice(0, width)]
+            for b in active:
+                d = step - LAG * b
+                if d == LAG and b + 1 < blocks:
+                    larger = centres[b + 1]
                 else:
-                    nc.scalar.copy(rounded[:], largest[h][:])
-                nc.tensor.matmul(products[h][:], weights[:, b, :], rounded[:], start=b == 0, stop=b == blocks - 1)
-        results = [held.tile([out_rows, half], F32, name=f"result{h}") for h in range(HALVES)]
-        nc.scalar.copy(results[0][:], products[0][:])
-        nc.scalar.dma_start(out[:, :half], results[0][:])
-        nc.vector.tensor_copy(results[1][:], products[1][:])
-        nc.sync.dma_start(out[:, half:], results[1][:])
+                    larger = held.tile([P, width], F32, name=f"larger{b}_{d}")
+                for cols in parts:
+                    entries = slice((d * width + cols.start) // STRIPE, (d * width + cols.stop) // STRIPE)
+                    picked = tables[b][:].indirect(offsets[:, entries])
+                    nc.vector.tensor_tensor(larger[:, cols], picked, largest[b][:, cols], mybir.AluOpType.max)
+                largest[b] = larger
+                if d < neighbours - 1:
+                    continue
+                rounded = held.tile([P, width], BF16, name=f"rounded{b}")
+                for h, cols in enumerate(halves):
+                    if b == blocks - 1 and h == HALVES - 1:
+                        nc.vector.tensor_copy(rounded[:, cols], larger[:, cols])
+                    else:
+                        nc.scalar.copy(rounded[:, cols], larger[:, cols])
+                    nc.tensor.matmul(
+                        products[h][:], weights[:, b, :], rounded[:, cols], start=b == 0, stop=b == blocks - 1
+                    )
+        result = held.tile([out_rows, width], F32, name="result")
+        nc.scalar.copy(result[:, halves[0]], products[0][:])
+        nc.scalar.dma_start(out[:, halves[0]], result[:, halves[0]])
+        nc.vector.tensor_copy(result[:, halves[1]], products[1][:])
+        nc.sync.dma_start(out[:, halves[1]], result[:, halves[1]])

@@ -5,7 +5,6 @@ STRIPE = 16
 F32, BF16, U16 = mybir.dt.float32, mybir.dt.bfloat16, mybir.dt.uint16
 FLOPS = 2 * 512 * 128 * 512
 HALVES = 2
-LAG = 2
 
 
 def tile_lookup_pool_max_none_kernel(tc, tab, x0, w, offs, out):
@@ -17,6 +16,8 @@ def tile_lookup_pool_max_none_kernel(tc, tab, x0, w, offs, out):
     neighbours = offs.shape[1] * STRIPE // width
     half = width // HALVES
     halves = [slice(h * half, (h + 1) * half) for h in range(HALVES)]
+    whole = [slice(0, width)]
+    groups = [[b] for b in range(blocks - 2)] + [[blocks - 2, blocks - 1]]
     with (
         tc.tile_pool(name="held", bufs=1) as held,
         tc.psum_pool(name="psum", bufs=1) as psum,
@@ -24,39 +25,36 @@ def tile_lookup_pool_max_none_kernel(tc, tab, x0, w, offs, out):
         offsets = held.tile([P, offs.shape[1]], U16, name="offsets")
         weights = held.tile([P, blocks, out_rows], BF16, name="weights")
         tables = [held.tile([P, table_cols], F32, name=f"table{b}") for b in range(blocks)]
-        centres = [held.tile([P, width], F32, name=f"centre{b}") for b in range(blocks)]
+        centres = held.tile([P, blocks, width], F32, name="centres")
+        x0_blocks = x0.rearrange("(b p) j -> p b j", p=P)
         nc.sync.dma_start(offsets[:], offs)
-        for b in range(blocks):
-            block_rows = slice(b * P, (b + 1) * P)
-            nc.sync.dma_start(tables[b][:], tab[block_rows, :])
-            nc.sync.dma_start(centres[b][:], x0[block_rows, :])
-            if b == 1:
+        for group in groups:
+            for b in group:
+                nc.sync.dma_start(tables[b][:], tab[b * P : (b + 1) * P, :])
+            members = slice(group[0], group[-1] + 1)
+            nc.sync.dma_start(centres[:, members, :], x0_blocks[:, members, :])
+            if 0 in group:
                 nc.sync.dma_start(weights[:], w.rearrange("(b p) m -> p b m", p=P))
 
         products = [psum.tile([out_rows, half], F32, name=f"product{h}") for h in range(HALVES)]
-        largest = list(centres)
-        for step in range(LAG * (blocks - 1) + neighbours):
-            active = [b for b in reversed(range(blocks)) if 0 <= step - LAG * b < neighbours]
-            parts = halves if len(active) == 1 else [slice(0, width)]
-            for b in active:
-                d = step - LAG * b
-                if d == LAG and b + 1 < blocks:
-                    larger = centres[b + 1]
-                else:
+        largest = [centres[:, b, :] for b in range(blocks)]
+        for group in groups:
+            for d in range(neighbours):
+                for b in group:
+                    last_step = b == blocks - 1 and d == neighbours - 1
                     larger = held.tile([P, width], F32, name=f"larger{b}_{d}")
-                for cols in parts:
-                    entries = slice((d * width + cols.start) // STRIPE, (d * width + cols.stop) // STRIPE)
-                    picked = tables[b][:].indirect(offsets[:, entries])
-                    nc.vector.tensor_tensor(larger[:, cols], picked, largest[b][:, cols], mybir.AluOpType.max)
-                largest[b] = larger
-                if d < neighbours - 1:
-                    continue
+                    for cols in halves if len(group) == 1 or last_step else whole:
+                        entries = slice((d * width + cols.start) // STRIPE, (d * width + cols.stop) // STRIPE)
+                        picked = tables[b][:].indirect(offsets[:, entries])
+                        nc.vector.tensor_tensor(larger[:, cols], picked, largest[b][:, cols], mybir.AluOpType.max)
+                    largest[b] = larger[:]
+            for b in group:
                 rounded = held.tile([P, width], BF16, name=f"rounded{b}")
                 for h, cols in enumerate(halves):
                     if b == blocks - 1 and h == HALVES - 1:
-                        nc.vector.tensor_copy(rounded[:, cols], larger[:, cols])
+                        nc.vector.tensor_copy(rounded[:, cols], largest[b][:, cols])
                     else:
-                        nc.scalar.copy(rounded[:, cols], larger[:, cols])
+                        nc.scalar.copy(rounded[:, cols], largest[b][:, cols])
                     nc.tensor.matmul(
                         products[h][:], weights[:, b, :], rounded[:, cols], start=b == 0, stop=b == blocks - 1
                     )

import concourse.mybir as mybir

P = 128
STRIPE = 16
F32, BF16, U16 = mybir.dt.float32, mybir.dt.bfloat16, mybir.dt.uint16
FLOPS = 2 * 512 * 128 * 512
HALVES = 2


def tile_lookup_pool_max_none_kernel(tc, tab, x0, w, offs, out):
    nc = tc.nc
    rows, table_cols = tab.shape
    width = x0.shape[1]
    out_rows = w.shape[1]
    blocks = rows // P
    neighbours = offs.shape[1] * STRIPE // width
    half = width // HALVES
    halves = [slice(h * half, (h + 1) * half) for h in range(HALVES)]
    whole = [slice(0, width)]
    groups = [[b] for b in range(blocks - 2)] + [[blocks - 2, blocks - 1]]
    with (
        tc.tile_pool(name="held", bufs=1) as held,
        tc.psum_pool(name="psum", bufs=1) as psum,
    ):
        offsets = held.tile([P, offs.shape[1]], U16, name="offsets")
        weights = held.tile([P, blocks, out_rows], BF16, name="weights")
        tables = [held.tile([P, table_cols], F32, name=f"table{b}") for b in range(blocks)]
        centres = held.tile([P, blocks, width], F32, name="centres")
        x0_blocks = x0.rearrange("(b p) j -> p b j", p=P)
        nc.sync.dma_start(offsets[:], offs)
        for group in groups:
            for b in group:
                nc.sync.dma_start(tables[b][:], tab[b * P : (b + 1) * P, :])
            members = slice(group[0], group[-1] + 1)
            nc.sync.dma_start(centres[:, members, :], x0_blocks[:, members, :])
            if 0 in group:
                nc.sync.dma_start(weights[:], w.rearrange("(b p) m -> p b m", p=P))

        products = [psum.tile([out_rows, half], F32, name=f"product{h}") for h in range(HALVES)]
        largest = [centres[:, b, :] for b in range(blocks)]
        for group in groups:
            for d in range(neighbours):
                for b in group:
                    last_step = b == blocks - 1 and d == neighbours - 1
                    larger = held.tile([P, width], F32, name=f"larger{b}_{d}")
                    for cols in halves if len(group) == 1 or last_step else whole:
                        entries = slice((d * width + cols.start) // STRIPE, (d * width + cols.stop) // STRIPE)
                        picked = tables[b][:].indirect(offsets[:, entries])
                        nc.vector.tensor_tensor(larger[:, cols], picked, largest[b][:, cols], mybir.AluOpType.max)
                    largest[b] = larger[:]
            for b in group:
                rounded = held.tile([P, width], BF16, name=f"rounded{b}")
                for h, cols in enumerate(halves):
                    if b == blocks - 1 and h == HALVES - 1:
                        nc.vector.tensor_copy(rounded[:, cols], largest[b][:, cols])
                    else:
                        nc.scalar.copy(rounded[:, cols], largest[b][:, cols])
                    nc.tensor.matmul(
                        products[h][:], weights[:, b, :], rounded[:, cols], start=b == 0, stop=b == blocks - 1
                    )
        result = held.tile([out_rows, width], F32, name="result")
        nc.scalar.copy(result[:, halves[0]], products[0][:])
        nc.scalar.dma_start(out[:, halves[0]], result[:, halves[0]])
        nc.vector.tensor_copy(result[:, halves[1]], products[1][:])
        nc.sync.dma_start(out[:, halves[1]], result[:, halves[1]])
